import numpy as np
import ml_dtypes


def mxq(x, axis, fmt="e4m3"):
    dtype, down = {"e4m3": (ml_dtypes.float8_e4m3fn, 7), "e5m2": (ml_dtypes.float8_e5m2, 14)}[fmt]
    v = np.moveaxis(np.asarray(x, np.float32).astype(ml_dtypes.bfloat16).astype(np.float64), axis, -1)
    blocks = v.reshape(v.shape[:-1] + (-1, 32))
    amax = np.abs(blocks).max(-1, keepdims=True)
    byte = np.maximum(np.where(amax > 0, np.frexp(amax)[1] - 1 + 127, 0) - down, 1)
    scale = np.exp2(byte - 127.0)
    codes = (blocks / scale).astype(np.float32).astype(dtype).astype(np.float64)
    return np.moveaxis((codes * scale).reshape(v.shape), -1, axis)


WIDE = False


def mx_kscale(k):
    if not WIDE:
        return np.ones(k)
    levels = np.array([24, -24, 12, -12, 0])
    if k % 512:
        return np.exp2(np.random.permutation(np.resize(levels, k // 32))).repeat(32)
    a = np.empty((k // 512, 16))
    for p in range(k // 512):
        a[p, :8] = np.random.permutation(np.resize(levels, 8))
        for g in range(8):
            far = levels[np.abs(levels - a[p, g]) >= 10]
            a[p, g + 8] = far[np.random.randint(len(far))]
    return np.exp2(a.ravel()).repeat(32)


def f64(x):
    return np.asarray(x).astype(np.float64)


def striped(idx):
    return np.tile(idx.reshape(-1, 16).T, (8, 1)).astype(np.uint16)


def unstriped(offs):
    return offs[:16].T.reshape(-1).astype(np.int64)


E2M1 = np.array([0.0, 0.5, 1.0, 1.5, 2.0, 3.0, 4.0, 6.0, -0.0, -0.5, -1.0, -1.5, -2.0, -3.0, -4.0, -6.0])


def pack_weight(w, fmt):
    k, n = w.shape
    w = f64(np.asarray(w, np.float32).astype(ml_dtypes.bfloat16)).reshape(k // 32, 32, n)
    amax = np.abs(w).max(1)
    if fmt == "e4m3":
        byte = np.frexp(amax)[1] - 1 + 127 - 7
    else:
        mant, ex = np.frexp(amax / 6.0)
        byte = np.where(mant > 0.5, ex, ex - 1) + 127
    byte = np.clip(np.where(amax > 0, byte, 1), 1, 254)
    scaled = (w * np.exp2(127.0 - byte)[:, None, :]).reshape(k, n).astype(np.float32)
    by_word = np.ascontiguousarray(scaled.reshape(k // 512, 128, 4, n).transpose(0, 1, 3, 2))
    if fmt == "e4m3":
        words = by_word.astype(ml_dtypes.float8_e4m3fn).view(np.uint8)
    else:
        c = by_word.astype(ml_dtypes.float4_e2m1fn).view(np.uint8) & 0xF
        words = (c[..., 0::2] | (c[..., 1::2] << 4)).reshape(k // 512, 128, 2 * n)
    return np.ascontiguousarray(words), np.ascontiguousarray(byte.astype(np.uint8).reshape(k // 512, 16, n))


def unpack_weight(words, scales, fmt):
    g, _, n = scales.shape
    words = np.ascontiguousarray(words).reshape(g, 128, n, -1)
    if fmt == "e4m3":
        vals = words.view(ml_dtypes.float8_e4m3fn).astype(np.float64)
    else:
        nib = np.empty((g, 128, n, 4), np.uint8)
        nib[..., 0::2] = words & 0xF
        nib[..., 1::2] = words >> 4
        vals = E2M1[nib]
    vals = vals * np.repeat(np.exp2(scales.astype(np.float64) - 127.0), 8, axis=1)[..., None]
    return vals.transpose(0, 1, 3, 2).reshape(g * 512, n)


def pack_table4(v):
    words, scales = pack_weight(v, "e2m1")
    g, t = words.shape[0] // 2, v.shape[1]
    return np.ascontiguousarray(words.reshape(g, 2, 128, t, 2).transpose(0, 2, 3, 1, 4).reshape(g, 128, t, 4)), scales


def unpack_table4(words, scales):
    g, _, t, _ = words.shape
    return unpack_weight(words.reshape(g, 128, t, 2, 2).transpose(0, 3, 1, 2, 4).reshape(2 * g, 128, 2 * t), scales, "e2m1")


K, R, N, T, J = 1024, 1024, 512, 4096, 2048


def setup_inputs():
    n = np.random.standard_normal
    s = mx_kscale(K)[:, None]
    u = mx_kscale(R)[:, None]
    wd = n((R, N)) / np.sqrt(R) / u
    p_tab = pack_table4(n((K, T)) * s)
    p_wg = pack_weight(n((K, R)) / np.sqrt(K) / s, "e4m3")
    p_wu = pack_weight(n((K, R)) / np.sqrt(K) / s * u.T, "e4m3")
    p_wd8 = pack_weight(wd[:512], "e4m3")
    p_wd4 = pack_weight(wd[512:], "e2m1")
    return {
        "tab_words": p_tab[0],
        "tab_scales": p_tab[1],
        "wg_words": p_wg[0],
        "wg_scales": p_wg[1],
        "wu_words": p_wu[0],
        "wu_scales": p_wu[1],
        "wd8_words": p_wd8[0],
        "wd8_scales": p_wd8[1],
        "wd4_words": p_wd4[0],
        "wd4_scales": p_wd4[1],
        "res": (n((N, J))).astype(np.float32),
        "offs": striped(np.random.permutation(T)[:J]),
    }


def reference(tab_words, tab_scales, wg_words, wg_scales, wu_words, wu_scales, wd8_words, wd8_scales, wd4_words, wd4_scales, res, offs):
    idx = unstriped(offs)
    tab_ = unpack_table4(tab_words, tab_scales)[:, idx]
    wg_ = unpack_weight(wg_words, wg_scales, "e4m3")
    wu_ = unpack_weight(wu_words, wu_scales, "e4m3")
    ga = wg_.T @ tab_
    ub = wu_.T @ tab_
    h = np.tanh(ga) * ub
    h_ = mxq(h, 0, "e4m3")
    wd8_ = unpack_weight(wd8_words, wd8_scales, "e4m3")
    wd4_ = unpack_weight(wd4_words, wd4_scales, "e2m1")
    y = wd8_.T @ h_[:512] + wd4_.T @ h_[512:]
    return f64(res) + y

@@ -1,0 +1,256 @@
+from contextlib import ExitStack
+
+import concourse.mybir as mybir
+
+K, R, N, T, J = 1024, 1024, 512, 4096, 2048
+FLOPS = 2 * J * (2 * K * R + R * N)
+
+F32 = mybir.dt.float32
+BF16 = mybir.dt.bfloat16
+I32 = mybir.dt.int32
+U32 = mybir.dt.uint32
+U16 = mybir.dt.uint16
+U8 = mybir.dt.uint8
+FP8X4 = mybir.dt.float8_e4m3fn_x4
+FP4X4 = mybir.dt.float4_e2m1fn_x4
+
+P = 128
+PACK = 4
+PASS = P * PACK
+CHUNK = 512
+SUB = 128
+CHUNKS = J // CHUNK
+SUBS = CHUNK // SUB
+HALVES = R // PASS
+LIVE = 96
+
+
+def tile_list_gmlpt_tanh_mix_res_kernel(
+    tc, tab_words, tab_scales, wg_words, wg_scales, wu_words, wu_scales,
+    wd8_words, wd8_scales, wd4_words, wd4_scales, res, offs, out,
+):
+    nc = tc.nc
+    mult, add = mybir.AluOpType.mult, mybir.AluOpType.add
+    tanh = mybir.ActivationFunctionType.Tanh
+
+    with ExitStack() as ctx:
+        keep = ctx.enter_context(tc.tile_pool(name="keep", bufs=1))
+        ring = ctx.enter_context(tc.tile_pool(name="ring", bufs=2))
+        psum = ctx.enter_context(tc.psum_pool(name="psum", bufs=8))
+
+        offsets = keep.tile([P, J // 16], U16, name="offsets")
+        nc.sync.dma_start(offsets[:], offs)
+
+        tab_rows = keep.tile([P, T], U8, name="tab_rows", align_bytes=64)
+        nc.vector.memset(tab_rows[0:LIVE, :].bitcast(I32), 0)
+        nc.sync.dma_start(tab_rows[LIVE:P, :].bitcast(I32), tab_scales.rearrange("a q t -> q a t").bitcast(I32))
+
+        w_rows = keep.tile([P, 2, R], U8, name="w_rows", tag="w_rows_then_wd8", align_bytes=64)
+        nc.vector.memset(w_rows[0:LIVE].rearrange("p w r -> p (w r)").bitcast(I32), 0)
+        for w, scales in enumerate((wg_scales, wu_scales)):
+            nc.sync.dma_start(w_rows[LIVE:P, w, :].bitcast(I32), scales.rearrange("a q r -> q a r").bitcast(I32))
+
+        table = keep.tile([P, T], U32, name="table", align_bytes=64)
+        nc.sync.dma_start(table[:].bitcast(I32), tab_words[0].rearrange("p t b -> p (t b)").bitcast(I32))
+
+        def list_slice(first_chunk, chunks):
+            cols = CHUNK // 16
+            return offsets[:, first_chunk * cols : (first_chunk + chunks) * cols]
+
+        def spread_rows(rows, width, name):
+            planes = keep.tile([P, 2, width], U8, name=name, align_bytes=64)
+            nc.vector.memset(planes[:].rearrange("p a c -> p (a c)").bitcast(I32), 0)
+            for quad in range(4):
+                nc.scalar.dma_start(
+                    planes[32 * quad : 32 * quad + 4].bitcast(I32),
+                    rows[LIVE + 8 * quad : LIVE + 8 * quad + 8, :].bitcast(I32),
+                )
+            return planes
+
+        tab_plane = {}
+        w_plane = {}
+
+        def early_planes(g):
+            picked = keep.tile([P, CHUNK], U8, name="picked_rows%d" % g, tag="picked_rows%d" % g, align_bytes=64)
+            nc.vector.tensor_copy(picked[:], tab_rows[:].indirect(list_slice(g, 1)))
+            rows = keep.tile([P, 3 * PASS], U8, name="rows%d" % g, tag="rows%d" % g, align_bytes=64)
+            nc.vector.tensor_copy(
+                rows[:, CHUNK:].rearrange("p (w t m) -> p w t m", w=2, t=PACK),
+                w_rows[:, :, g * PASS : (g + 1) * PASS].rearrange("p w (m t) -> p w t m", t=PACK),
+            )
+            nc.vector.tensor_copy(rows[:, 0:CHUNK].bitcast(I32), picked[:].bitcast(I32))
+            planes = spread_rows(rows, 3 * PASS, "planes%d" % g)
+            tab_plane[g] = planes[:, :, 0:CHUNK]
+            for w in range(2):
+                w_plane[w, g] = planes[:, :, CHUNK + w * PASS : CHUNK + (w + 1) * PASS]
+
+        def late_planes():
+            picked = keep.tile([P, 2 * CHUNK], U8, name="picked_rows2", tag="rows1", align_bytes=64)
+            nc.vector.tensor_copy(picked[:], tab_rows[:].indirect(list_slice(2, 2)))
+            planes = spread_rows(picked, 2 * CHUNK, "planes2")
+            for c in (2, 3):
+                tab_plane[c] = planes[:, :, (c - 2) * CHUNK : (c - 1) * CHUNK]
+
+        w_codes = {}
+
+        def load_weights(w, half):
+            words = (wg_words, wu_words)[w]
+            raw = ring.tile([P, 2, PASS], I32, name="raw", tag="stream")
+            src = words.rearrange("a p r i -> p a (r i)")[:, :, half * PASS * 4 : (half + 1) * PASS * 4]
+            nc.sync.dma_start(raw[:], src.bitcast(I32))
+            codes = keep.tile([P, 2, PASS], I32, name="w_codes%d%d" % (w, half), align_bytes=64)
+            nc.vector.tensor_copy(
+                codes[:].rearrange("p a (t g i) -> p a g t i", t=PACK, i=4),
+                raw[:].rearrange("p a (g i t) -> p a g t i", t=PACK, i=4),
+            )
+            w_codes[w, half] = codes
+
+        tab_codes = {}
+
+        def pick_words(c):
+            picked = keep.tile([P, CHUNK], U32, name="picked_words", tag="rows1" if c > 0 else "picked_words0", align_bytes=64)
+            nc.vector.tensor_copy(picked[:], table[:].indirect(list_slice(c, 1)))
+            parted = ring.tile([P, 2, 2 * CHUNK], U8, name="parted", align_bytes=64)
+            nc.vector.tensor_copy(parted[:].bitcast(U16), picked[:].bitcast(U16).rearrange("p (j a) -> p a j", a=2))
+            tab_codes[c] = parted
+
+        wd = {}
+
+        def load_down():
+            wd8 = keep.tile([P, N], I32, name="wd8", tag="w_rows_then_wd8", align_bytes=64)
+            nc.sync.dma_start(wd8[:], wd8_words[0].rearrange("p n i -> p (n i)").bitcast(I32))
+            wd4 = keep.tile([P, 2 * N], U8, name="wd4", tag="picked_rows1", align_bytes=64)
+            nc.sync.dma_start(wd4[:].bitcast(I32), wd4_words[0].bitcast(I32))
+            planes = keep.tile([P, 2, N], U8, name="wd_planes", tag="rows0", align_bytes=64)
+            nc.vector.memset(planes[:].rearrange("p a c -> p (a c)").bitcast(I32), 0)
+            for half, scales in enumerate((wd8_scales, wd4_scales)):
+                for quad in range(4):
+                    nc.sync.dma_start(
+                        planes[32 * quad : 32 * quad + 4, half, :].bitcast(I32),
+                        scales[0, 4 * quad : 4 * quad + 4, :].bitcast(I32),
+                    )
+            wd["codes"] = (wd8, wd4)
+            wd["planes"] = planes
+
+        res_tiles = {}
+
+        def load_res(c):
+            tile = ring.tile([P, N // P, CHUNK], F32, name="res_tile", tag="stream")
+            nc.sync.dma_start(tile[:], res[:, c * CHUNK : (c + 1) * CHUNK].rearrange("(b p) j -> p b j", p=P))
+            res_tiles[c] = tile
+
+        def first_product(dst, w, half, t, c, j0, width):
+            for a in range(2):
+                nc.tensor.matmul_mx(
+                    out=dst,
+                    lhsT=w_codes[w, half][:, a, t * P : (t + 1) * P].bitcast(FP8X4),
+                    lhsT_scale=w_plane[w, half][:, a, t * P : (t + 1) * P],
+                    rhs=tab_codes[c][:, a, 2 * j0 : 2 * (j0 + width)].bitcast(FP4X4),
+                    rhs_scale=tab_plane[c][:, a, j0 : j0 + width],
+                    start=(a == 0),
+                    stop=(a == 1),
+                )
+
+        def gate(c, half):
+            gates = ring.tile([P, PACK, CHUNK], F32, name="gates")
+            for t in range(PACK):
+                bank = psum.tile([P, CHUNK], F32, name="bank")
+                first_product(bank[:], 0, half, t, c, 0, CHUNK)
+                nc.scalar.activation(gates[:, t, :], bank[:], tanh)
+            return gates
+
+        def up_times_gate(c, half, s, gates, h):
+            bank = psum.tile([P, CHUNK], F32, name="bank")
+            for t in range(PACK):
+                first_product(bank[:, t * SUB : (t + 1) * SUB], 1, half, t, c, s * SUB, SUB)
+            nc.vector.tensor_tensor(
+                h[:, s * SUB * PACK : (s + 1) * SUB * PACK].rearrange("p (g i t) -> p g t i", t=PACK, i=2),
+                bank[:].rearrange("p (t g i) -> p g t i", t=PACK, i=2),
+                gates[:, :, s * SUB : (s + 1) * SUB].rearrange("p t (g i) -> p g t i", i=2),
+                mult,
+            )
+
+        h_codes = {}
+
+        def new_h(c, half):
+            h = ring.tile([P, CHUNK * PACK], BF16, name="h", align_bytes=64)
+            codes = ring.tile([P, CHUNK], U32, name="h_words", tag="h_words%d" % half, align_bytes=64)
+            scales = ring.tile([P, CHUNK], U8, name="h_scales", tag="h_scales%d" % half, align_bytes=64)
+            h_codes[c, half] = (codes, scales)
+            return h
+
+        def quantise(c, half, h, j0, width):
+            codes, scales = h_codes[c, half]
+            nc.vector.quantize_mx(
+                out=codes[:, j0 : j0 + width].bitcast(FP8X4),
+                scales=scales[:, j0 : j0 + width],
+                in_=h[:, j0 * PACK : (j0 + width) * PACK],
+            )
+
+        def second_product(dst, c, b, j0, width):
+            wd8, wd4 = wd["codes"]
+            stationary = (wd8[:, b * P : (b + 1) * P].bitcast(FP8X4), wd4[:, 2 * b * P : 2 * (b + 1) * P].bitcast(FP4X4))
+            for half in range(HALVES):
+                codes, scales = h_codes[c, half]
+                nc.tensor.matmul_mx(
+                    out=dst,
+                    lhsT=stationary[half],
+                    lhsT_scale=wd["planes"][:, half, b * P : (b + 1) * P],
+                    rhs=codes[:, j0 : j0 + width].bitcast(FP8X4),
+                    rhs_scale=scales[:, j0 : j0 + width],
+                    start=(half == 0),
+                    stop=(half == HALVES - 1),
+                )
+
+        def down(c):
+            for b in range(N // P):
+                bank = psum.tile([P, CHUNK], F32, name="bank")
+                second_product(bank[:], c, b, 0, CHUNK)
+                result = ring.tile([P, CHUNK], F32, name="result", bufs=4)
+                nc.vector.tensor_tensor(result[:], bank[:], res_tiles[c][:, b, :], add)
+                nc.sync.dma_start(out[b * P : (b + 1) * P, c * CHUNK : (c + 1) * CHUNK], result[:])
+
+        def down_sub(c, s):
+            bank = psum.tile([P, CHUNK], F32, name="bank")
+            for b in range(N // P):
+                second_product(bank[:, b * SUB : (b + 1) * SUB], c, b, s * SUB, SUB)
+            result = ring.tile([P, CHUNK], F32, name="result", bufs=4)
+            by_block = result[:].rearrange("p (b j) -> p b j", j=SUB)
+            nc.vector.tensor_tensor(
+                by_block, bank[:].rearrange("p (b j) -> p b j", j=SUB), res_tiles[c][:, :, s * SUB : (s + 1) * SUB], add
+            )
+            j0 = c * CHUNK + s * SUB
+            nc.sync.dma_start(out[:, j0 : j0 + SUB].rearrange("(b p) j -> p b j", p=P), by_block)
+
+        early_planes(0)
+        early_planes(1)
+        pick_words(0)
+        load_weights(0, 0)
+        load_weights(1, 0)
+        load_weights(0, 1)
+        load_weights(1, 1)
+        load_down()
+
+        for c in range(CHUNKS):
+            last = c == CHUNKS - 1
+            load_res(c)
+            for half in range(HALVES):
+                gates = gate(c, half)
+                if half == 0 and c > 0:
+                    down(c - 1)
+                if half == 1 and not last:
+                    pick_words(c + 1)
+                h = new_h(c, half)
+                if last and half == 1:
+                    for s in range(SUBS + 2):
+                        if s < SUBS:
+                            up_times_gate(c, half, s, gates, h)
+                            quantise(c, half, h, s * SUB, SUB)
+                        if s >= 2:
+                            down_sub(c, s - 2)
+                else:
+                    for s in range(SUBS):
+                        up_times_gate(c, half, s, gates, h)
+                    quantise(c, half, h, 0, CHUNK)
+                if c == 0 and half == 1:
+                    late_planes()

@@ -41,14 +41,14 @@ def tile_list_gmlpt_tanh_mix_res_kernel(
         offsets = keep.tile([P, J // 16], U16, name="offsets")
         nc.sync.dma_start(offsets[:], offs)
 
-        tab_rows = keep.tile([P, T], U8, name="tab_rows", align_bytes=64)
-        nc.vector.memset(tab_rows[0:LIVE, :].bitcast(I32), 0)
-        nc.sync.dma_start(tab_rows[LIVE:P, :].bitcast(I32), tab_scales.rearrange("a q t -> q a t").bitcast(I32))
-
-        w_rows = keep.tile([P, 2, R], U8, name="w_rows", tag="w_rows_then_wd8", align_bytes=64)
+        w_rows = keep.tile([P, 2, R], U8, name="w_rows", tag="stream2", align_bytes=64)
         nc.vector.memset(w_rows[0:LIVE].rearrange("p w r -> p (w r)").bitcast(I32), 0)
         for w, scales in enumerate((wg_scales, wu_scales)):
             nc.sync.dma_start(w_rows[LIVE:P, w, :].bitcast(I32), scales.rearrange("a q r -> q a r").bitcast(I32))
+
+        tab_rows = keep.tile([P, T], U8, name="tab_rows", align_bytes=64)
+        nc.vector.memset(tab_rows[0:LIVE, :].bitcast(I32), 0)
+        nc.sync.dma_start(tab_rows[LIVE:P, :].bitcast(I32), tab_scales.rearrange("a q t -> q a t").bitcast(I32))
 
         table = keep.tile([P, T], U32, name="table", align_bytes=64)
         nc.sync.dma_start(table[:].bitcast(I32), tab_words[0].rearrange("p t b -> p (t b)").bitcast(I32))
@@ -57,11 +57,11 @@ def tile_list_gmlpt_tanh_mix_res_kernel(
             cols = CHUNK // 16
             return offsets[:, first_chunk * cols : (first_chunk + chunks) * cols]
 
-        def spread_rows(rows, width, name):
+        def spread_rows(rows, width, name, queue):
             planes = keep.tile([P, 2, width], U8, name=name, align_bytes=64)
             nc.vector.memset(planes[:].rearrange("p a c -> p (a c)").bitcast(I32), 0)
             for quad in range(4):
-                nc.scalar.dma_start(
+                queue.dma_start(
                     planes[32 * quad : 32 * quad + 4].bitcast(I32),
                     rows[LIVE + 8 * quad : LIVE + 8 * quad + 8, :].bitcast(I32),
                 )
@@ -69,73 +69,80 @@ def tile_list_gmlpt_tanh_mix_res_kernel(
 
         tab_plane = {}
         w_plane = {}
+        wd = {}
 
-        def early_planes(g):
-            picked = keep.tile([P, CHUNK], U8, name="picked_rows%d" % g, tag="picked_rows%d" % g, align_bytes=64)
-            nc.vector.tensor_copy(picked[:], tab_rows[:].indirect(list_slice(g, 1)))
-            rows = keep.tile([P, 3 * PASS], U8, name="rows%d" % g, tag="rows%d" % g, align_bytes=64)
+        def order_scale_rows(dst, half):
             nc.vector.tensor_copy(
-                rows[:, CHUNK:].rearrange("p (w t m) -> p w t m", w=2, t=PACK),
-                w_rows[:, :, g * PASS : (g + 1) * PASS].rearrange("p w (m t) -> p w t m", t=PACK),
+                dst.rearrange("p (w t m) -> p w t m", w=2, t=PACK),
+                w_rows[:, :, half * PASS : (half + 1) * PASS].rearrange("p w (m t) -> p w t m", t=PACK),
             )
-            nc.vector.tensor_copy(rows[:, 0:CHUNK].bitcast(I32), picked[:].bitcast(I32))
-            planes = spread_rows(rows, 3 * PASS, "planes%d" % g)
-            tab_plane[g] = planes[:, :, 0:CHUNK]
+
+        def first_planes():
+            rows = keep.tile([P, 2 * PASS + CHUNK], U8, name="rows0", tag="rows0", align_bytes=64)
+            order_scale_rows(rows[:, 0 : 2 * PASS], 0)
+            picked = keep.tile([P, CHUNK], U8, name="picked_rows0", tag="scratch", align_bytes=64)
+            nc.vector.tensor_copy(picked[:], tab_rows[:].indirect(list_slice(0, 1)))
+            nc.vector.tensor_copy(rows[:, 2 * PASS :].bitcast(I32), picked[:].bitcast(I32))
+            planes = spread_rows(rows, 2 * PASS + CHUNK, "planes0", nc.scalar)
+            tab_plane[0] = planes[:, :, 2 * PASS :]
             for w in range(2):
-                w_plane[w, g] = planes[:, :, CHUNK + w * PASS : CHUNK + (w + 1) * PASS]
+                w_plane[w, 0] = planes[:, :, w * PASS : (w + 1) * PASS]
+
+        def second_planes():
+            rows = keep.tile([P, 2 * PASS], U8, name="rows1", tag="scratch", align_bytes=64)
+            order_scale_rows(rows[:], 1)
+            planes = spread_rows(rows, 2 * PASS, "planes1", nc.sync)
+            for w in range(2):
+                w_plane[w, 1] = planes[:, :, w * PASS : (w + 1) * PASS]
 
         def late_planes():
-            picked = keep.tile([P, 2 * CHUNK], U8, name="picked_rows2", tag="rows1", align_bytes=64)
-            nc.vector.tensor_copy(picked[:], tab_rows[:].indirect(list_slice(2, 2)))
-            planes = spread_rows(picked, 2 * CHUNK, "planes2")
-            for c in (2, 3):
-                tab_plane[c] = planes[:, :, (c - 2) * CHUNK : (c - 1) * CHUNK]
+            width = (CHUNKS - 1) * CHUNK
+            picked = keep.tile([P, width], U8, name="picked_rows1", tag="stream1", align_bytes=64)
+            nc.vector.tensor_copy(picked[:], tab_rows[:].indirect(list_slice(1, CHUNKS - 1)))
+            rows = keep.tile([P, width + N], U8, name="rows2", tag="rows0", align_bytes=64)
+            for half, scales in enumerate((wd8_scales, wd4_scales)):
+                nc.sync.dma_start(rows[LIVE + half : P : 2, width:].bitcast(I32), scales[0].bitcast(I32))
+            nc.vector.tensor_copy(rows[:, 0:width].bitcast(I32), picked[:].bitcast(I32))
+            planes = spread_rows(rows, width + N, "planes2", nc.sync)
+            wd["planes"] = planes[:, :, width:]
+            for c in range(1, CHUNKS):
+                tab_plane[c] = planes[:, :, (c - 1) * CHUNK : c * CHUNK]
 
         w_codes = {}
 
-        def load_weights(w, half):
+        def load_weights(w, half, raw):
             words = (wg_words, wu_words)[w]
-            raw = ring.tile([P, 2, PASS], I32, name="raw", tag="stream")
             src = words.rearrange("a p r i -> p a (r i)")[:, :, half * PASS * 4 : (half + 1) * PASS * 4]
-            nc.sync.dma_start(raw[:], src.bitcast(I32))
+            nc.sync.dma_start(raw, src.bitcast(I32))
+
+        def order_weights(w, half, raw):
             codes = keep.tile([P, 2, PASS], I32, name="w_codes%d%d" % (w, half), align_bytes=64)
             nc.vector.tensor_copy(
                 codes[:].rearrange("p a (t g i) -> p a g t i", t=PACK, i=4),
-                raw[:].rearrange("p a (g i t) -> p a g t i", t=PACK, i=4),
+                raw.rearrange("p a (g i t) -> p a g t i", t=PACK, i=4),
             )
             w_codes[w, half] = codes
 
         tab_codes = {}
 
         def pick_words(c):
-            picked = keep.tile([P, CHUNK], U32, name="picked_words", tag="rows1" if c > 0 else "picked_words0", align_bytes=64)
+            picked = keep.tile([P, CHUNK], U32, name="picked_words", tag="stream2" if c > 0 else "picked_words0", align_bytes=64)
             nc.vector.tensor_copy(picked[:], table[:].indirect(list_slice(c, 1)))
             parted = ring.tile([P, 2, 2 * CHUNK], U8, name="parted", align_bytes=64)
             nc.vector.tensor_copy(parted[:].bitcast(U16), picked[:].bitcast(U16).rearrange("p (j a) -> p a j", a=2))
             tab_codes[c] = parted
 
-        wd = {}
-
         def load_down():
-            wd8 = keep.tile([P, N], I32, name="wd8", tag="w_rows_then_wd8", align_bytes=64)
-            nc.sync.dma_start(wd8[:], wd8_words[0].rearrange("p n i -> p (n i)").bitcast(I32))
-            wd4 = keep.tile([P, 2 * N], U8, name="wd4", tag="picked_rows1", align_bytes=64)
-            nc.sync.dma_start(wd4[:].bitcast(I32), wd4_words[0].bitcast(I32))
-            planes = keep.tile([P, 2, N], U8, name="wd_planes", tag="rows0", align_bytes=64)
-            nc.vector.memset(planes[:].rearrange("p a c -> p (a c)").bitcast(I32), 0)
-            for half, scales in enumerate((wd8_scales, wd4_scales)):
-                for quad in range(4):
-                    nc.sync.dma_start(
-                        planes[32 * quad : 32 * quad + 4, half, :].bitcast(I32),
-                        scales[0, 4 * quad : 4 * quad + 4, :].bitcast(I32),
-                    )
+            words = keep.tile([P, 6 * N], U8, name="wd_words", tag="picked_words0", align_bytes=64)
+            wd8, wd4 = words[:, 0 : 4 * N], words[:, 4 * N :]
+            nc.sync.dma_start(wd8.bitcast(I32), wd8_words[0].rearrange("p n i -> p (n i)").bitcast(I32))
+            nc.sync.dma_start(wd4.bitcast(I32), wd4_words[0].bitcast(I32))
             wd["codes"] = (wd8, wd4)
-            wd["planes"] = planes
 
         res_tiles = {}
 
         def load_res(c):
-            tile = ring.tile([P, N // P, CHUNK], F32, name="res_tile", tag="stream")
+            tile = keep.tile([P, N // P, CHUNK], F32, name="res_tile", tag="stream%d" % (c % 2), align_bytes=64)
             nc.sync.dma_start(tile[:], res[:, c * CHUNK : (c + 1) * CHUNK].rearrange("(b p) j -> p b j", p=P))
             res_tiles[c] = tile
 
@@ -170,6 +177,19 @@ def tile_list_gmlpt_tanh_mix_res_kernel(
                 mult,
             )
 
+        def up_then_product(c, half, gates, h):
+            ups = ring.tile([P, PACK, CHUNK], F32, name="ups")
+            for t in range(PACK):
+                bank = psum.tile([P, CHUNK], F32, name="bank")
+                first_product(bank[:], 1, half, t, c, 0, CHUNK)
+                nc.scalar.copy(ups[:, t, :], bank[:])
+            nc.vector.tensor_tensor(
+                h[:].rearrange("p (g i t) -> p g t i", t=PACK, i=2),
+                ups[:].rearrange("p t (g i) -> p g t i", i=2),
+                gates[:].rearrange("p t (g i) -> p g t i", i=2),
+                mult,
+            )
+
         h_codes = {}
 
         def new_h(c, half):
@@ -189,7 +209,7 @@ def tile_list_gmlpt_tanh_mix_res_kernel(
 
         def second_product(dst, c, b, j0, width):
             wd8, wd4 = wd["codes"]
-            stationary = (wd8[:, b * P : (b + 1) * P].bitcast(FP8X4), wd4[:, 2 * b * P : 2 * (b + 1) * P].bitcast(FP4X4))
+            stationary = (wd8[:, 4 * b * P : 4 * (b + 1) * P].bitcast(FP8X4), wd4[:, 2 * b * P : 2 * (b + 1) * P].bitcast(FP4X4))
             for half in range(HALVES):
                 codes, scales = h_codes[c, half]
                 nc.tensor.matmul_mx(
@@ -222,13 +242,21 @@ def tile_list_gmlpt_tanh_mix_res_kernel(
             j0 = c * CHUNK + s * SUB
             nc.sync.dma_start(out[:, j0 : j0 + SUB].rearrange("(b p) j -> p b j", p=P), by_block)
 
-        early_planes(0)
-        early_planes(1)
+        raw_gate0 = keep.tile([P, 2, PASS], I32, name="raw_gate0", tag="stream0", align_bytes=64)
+        load_weights(0, 0, raw_gate0[:])
+        raw_up0 = keep.tile([P, 2, PASS], I32, name="raw_up0", tag="stream1", align_bytes=64)
+        load_weights(1, 0, raw_up0[:])
+        first_planes()
+        second_planes()
+        raw1 = keep.tile([P, 2, 2, PASS], I32, name="raw1", tag="stream2", align_bytes=64)
+        for w in range(2):
+            load_weights(w, 1, raw1[:, w])
         pick_words(0)
-        load_weights(0, 0)
-        load_weights(1, 0)
-        load_weights(0, 1)
-        load_weights(1, 1)
+        order_weights(0, 0, raw_gate0[:])
+        order_weights(1, 0, raw_up0[:])
+        for w in range(2):
+            order_weights(w, 1, raw1[:, w])
+        late_planes()
         load_down()
 
         for c in range(CHUNKS):
@@ -236,7 +264,7 @@ def tile_list_gmlpt_tanh_mix_res_kernel(
             load_res(c)
             for half in range(HALVES):
                 gates = gate(c, half)
-                if half == 0 and c > 0:
+                if half == 1 and c > 0:
                     down(c - 1)
                 if half == 1 and not last:
                     pick_words(c + 1)
@@ -249,8 +277,5 @@ def tile_list_gmlpt_tanh_mix_res_kernel(
                         if s >= 2:
                             down_sub(c, s - 2)
                 else:
-                    for s in range(SUBS):
-                        up_times_gate(c, half, s, gates, h)
+                    up_then_product(c, half, gates, h)
                     quantise(c, half, h, 0, CHUNK)
-                if c == 0 and half == 1:
-                    late_planes()

@@ -22,6 +22,10 @@ SUB = 128
 CHUNKS = J // CHUNK
 SUBS = CHUNK // SUB
 HALVES = R // PASS
+RES_BYTES = 4 * (N // P) * CHUNK
+RAW_BYTES = 4 * 2 * PASS
+ROWS1_AT = RES_BYTES
+RES_AT = (0, ROWS1_AT + 2 * PASS)
 LIVE = 96
 
 
@@ -36,6 +40,7 @@ def tile_list_gmlpt_tanh_mix_res_kernel(
     with ExitStack() as ctx:
         keep = ctx.enter_context(tc.tile_pool(name="keep", bufs=1))
         ring = ctx.enter_context(tc.tile_pool(name="ring", bufs=2))
+        placed = ctx.enter_context(tc.tile_pool(name="placed", bufs=1))
         psum = ctx.enter_context(tc.psum_pool(name="psum", bufs=8))
 
         offsets = keep.tile([P, J // 16], U16, name="offsets")
@@ -57,11 +62,11 @@ def tile_list_gmlpt_tanh_mix_res_kernel(
             cols = CHUNK // 16
             return offsets[:, first_chunk * cols : (first_chunk + chunks) * cols]
 
-        def spread_rows(rows, width, name, queue):
+        def spread_rows(rows, width, name, clearer):
             planes = keep.tile([P, 2, width], U8, name=name, align_bytes=64)
-            nc.vector.memset(planes[:].rearrange("p a c -> p (a c)").bitcast(I32), 0)
+            clearer.memset(planes[:].rearrange("p a c -> p (a c)").bitcast(I32), 0)
             for quad in range(4):
-                queue.dma_start(
+                nc.sync.dma_start(
                     planes[32 * quad : 32 * quad + 4].bitcast(I32),
                     rows[LIVE + 8 * quad : LIVE + 8 * quad + 8, :].bitcast(I32),
                 )
@@ -80,30 +85,31 @@ def tile_list_gmlpt_tanh_mix_res_kernel(
         def first_planes():
             rows = keep.tile([P, 2 * PASS + CHUNK], U8, name="rows0", tag="rows0", align_bytes=64)
             order_scale_rows(rows[:, 0 : 2 * PASS], 0)
-            picked = keep.tile([P, CHUNK], U8, name="picked_rows0", tag="scratch", align_bytes=64)
-            nc.vector.tensor_copy(picked[:], tab_rows[:].indirect(list_slice(0, 1)))
-            nc.vector.tensor_copy(rows[:, 2 * PASS :].bitcast(I32), picked[:].bitcast(I32))
-            planes = spread_rows(rows, 2 * PASS + CHUNK, "planes0", nc.scalar)
+            span = placed.tile([P, 2 * PASS + 128], U8, name="picked_rows0", offset=ROWS1_AT - 64, align_bytes=64)
+            picked = span[:, 0:CHUNK]
+            nc.vector.tensor_copy(picked, tab_rows[:].indirect(list_slice(0, 1)))
+            nc.vector.tensor_copy(rows[:, 2 * PASS :].bitcast(I32), picked.bitcast(I32))
+            planes = spread_rows(rows, 2 * PASS + CHUNK, "planes0", nc.vector)
             tab_plane[0] = planes[:, :, 2 * PASS :]
             for w in range(2):
                 w_plane[w, 0] = planes[:, :, w * PASS : (w + 1) * PASS]
 
         def second_planes():
-            rows = keep.tile([P, 2 * PASS], U8, name="rows1", tag="scratch", align_bytes=64)
+            rows = placed.tile([P, 2 * PASS], U8, name="rows1", offset=ROWS1_AT, align_bytes=64)
             order_scale_rows(rows[:], 1)
-            planes = spread_rows(rows, 2 * PASS, "planes1", nc.sync)
+            planes = spread_rows(rows, 2 * PASS, "planes1", nc.gpsimd)
             for w in range(2):
                 w_plane[w, 1] = planes[:, :, w * PASS : (w + 1) * PASS]
 
         def late_planes():
             width = (CHUNKS - 1) * CHUNK
-            picked = keep.tile([P, width], U8, name="picked_rows1", tag="stream1", align_bytes=64)
+            picked = placed.tile([P, width], U8, name="picked_rows1", offset=RES_AT[1], align_bytes=64)
             nc.vector.tensor_copy(picked[:], tab_rows[:].indirect(list_slice(1, CHUNKS - 1)))
             rows = keep.tile([P, width + N], U8, name="rows2", tag="rows0", align_bytes=64)
             for half, scales in enumerate((wd8_scales, wd4_scales)):
                 nc.sync.dma_start(rows[LIVE + half : P : 2, width:].bitcast(I32), scales[0].bitcast(I32))
             nc.vector.tensor_copy(rows[:, 0:width].bitcast(I32), picked[:].bitcast(I32))
-            planes = spread_rows(rows, width + N, "planes2", nc.sync)
+            planes = spread_rows(rows, width + N, "planes2", nc.gpsimd)
             wd["planes"] = planes[:, :, width:]
             for c in range(1, CHUNKS):
                 tab_plane[c] = planes[:, :, (c - 1) * CHUNK : c * CHUNK]
@@ -115,13 +121,15 @@ def tile_list_gmlpt_tanh_mix_res_kernel(
             src = words.rearrange("a p r i -> p a (r i)")[:, :, half * PASS * 4 : (half + 1) * PASS * 4]
             nc.sync.dma_start(raw, src.bitcast(I32))
 
-        def order_weights(w, half, raw):
-            codes = keep.tile([P, 2, PASS], I32, name="w_codes%d%d" % (w, half), align_bytes=64)
+        def order_weights(w, half, raw, a0):
+            passes = raw.shape[1]
+            codes = keep.tile([P, passes, PASS], I32, name="w_codes%d%d%d" % (w, half, a0), align_bytes=64)
             nc.vector.tensor_copy(
                 codes[:].rearrange("p a (t g i) -> p a g t i", t=PACK, i=4),
                 raw.rearrange("p a (g i t) -> p a g t i", t=PACK, i=4),
             )
-            w_codes[w, half] = codes
+            for a in range(passes):
+                w_codes[w, half, a0 + a] = codes[:, a, :]
 
         tab_codes = {}
 
@@ -142,7 +150,7 @@ def tile_list_gmlpt_tanh_mix_res_kernel(
         res_tiles = {}
 
         def load_res(c):
-            tile = keep.tile([P, N // P, CHUNK], F32, name="res_tile", tag="stream%d" % (c % 2), align_bytes=64)
+            tile = placed.tile([P, N // P, CHUNK], F32, name="res_tile", tag="res%d" % (c % 2), offset=RES_AT[c % 2], align_bytes=64)
             nc.sync.dma_start(tile[:], res[:, c * CHUNK : (c + 1) * CHUNK].rearrange("(b p) j -> p b j", p=P))
             res_tiles[c] = tile
 
@@ -150,7 +158,7 @@ def tile_list_gmlpt_tanh_mix_res_kernel(
             for a in range(2):
                 nc.tensor.matmul_mx(
                     out=dst,
-                    lhsT=w_codes[w, half][:, a, t * P : (t + 1) * P].bitcast(FP8X4),
+                    lhsT=w_codes[w, half, a][:, t * P : (t + 1) * P].bitcast(FP8X4),
                     lhsT_scale=w_plane[w, half][:, a, t * P : (t + 1) * P],
                     rhs=tab_codes[c][:, a, 2 * j0 : 2 * (j0 + width)].bitcast(FP4X4),
                     rhs_scale=tab_plane[c][:, a, j0 : j0 + width],
@@ -234,28 +242,32 @@ def tile_list_gmlpt_tanh_mix_res_kernel(
             bank = psum.tile([P, CHUNK], F32, name="bank")
             for b in range(N // P):
                 second_product(bank[:, b * SUB : (b + 1) * SUB], c, b, s * SUB, SUB)
-            result = ring.tile([P, CHUNK], F32, name="result", bufs=4)
-            by_block = result[:].rearrange("p (b j) -> p b j", j=SUB)
-            nc.vector.tensor_tensor(
-                by_block, bank[:].rearrange("p (b j) -> p b j", j=SUB), res_tiles[c][:, :, s * SUB : (s + 1) * SUB], add
-            )
             j0 = c * CHUNK + s * SUB
-            nc.sync.dma_start(out[:, j0 : j0 + SUB].rearrange("(b p) j -> p b j", p=P), by_block)
+            sums = bank[:].rearrange("p (b j) -> p b j", j=SUB)
+            stored = out[:, j0 : j0 + SUB].rearrange("(b p) j -> p b j", p=P)
+            queues = (nc.sync, nc.scalar) if s == SUBS - 1 else (nc.sync,)
+            blocks = N // P // len(queues)
+            for n, queue in enumerate(queues):
+                part = slice(n * blocks, (n + 1) * blocks)
+                result = ring.tile([P, blocks, SUB], F32, name="result", bufs=4)
+                nc.vector.tensor_tensor(result[:], sums[:, part], res_tiles[c][:, part, s * SUB : (s + 1) * SUB], add)
+                queue.dma_start(stored[:, part], result[:])
 
-        raw_gate0 = keep.tile([P, 2, PASS], I32, name="raw_gate0", tag="stream0", align_bytes=64)
-        load_weights(0, 0, raw_gate0[:])
-        raw_up0 = keep.tile([P, 2, PASS], I32, name="raw_up0", tag="stream1", align_bytes=64)
-        load_weights(1, 0, raw_up0[:])
         first_planes()
+        raw_gate0 = placed.tile([P, 2, PASS], I32, name="raw_gate0", offset=RES_BYTES - RAW_BYTES, align_bytes=64)
+        load_weights(0, 0, raw_gate0[:])
+        raw_up0 = placed.tile([P, 2, PASS], I32, name="raw_up0", offset=RES_AT[1], align_bytes=64)
+        load_weights(1, 0, raw_up0[:])
         second_planes()
         raw1 = keep.tile([P, 2, 2, PASS], I32, name="raw1", tag="stream2", align_bytes=64)
         for w in range(2):
             load_weights(w, 1, raw1[:, w])
         pick_words(0)
-        order_weights(0, 0, raw_gate0[:])
-        order_weights(1, 0, raw_up0[:])
+        for a in range(2):
+            order_weights(0, 0, raw_gate0[:, a : a + 1, :], a)
+        order_weights(1, 0, raw_up0[:], 0)
         for w in range(2):
-            order_weights(w, 1, raw1[:, w])
+            order_weights(w, 1, raw1[:, w], 0)
         late_planes()
         load_down()
 

from contextlib import ExitStack

import concourse.mybir as mybir

K, R, N, T, J = 1024, 1024, 512, 4096, 2048
FLOPS = 2 * J * (2 * K * R + R * N)

F32 = mybir.dt.float32
BF16 = mybir.dt.bfloat16
I32 = mybir.dt.int32
U32 = mybir.dt.uint32
U16 = mybir.dt.uint16
U8 = mybir.dt.uint8
FP8X4 = mybir.dt.float8_e4m3fn_x4
FP4X4 = mybir.dt.float4_e2m1fn_x4

P = 128
PACK = 4
PASS = P * PACK
CHUNK = 512
SUB = 128
CHUNKS = J // CHUNK
SUBS = CHUNK // SUB
HALVES = R // PASS
RES_BYTES = 4 * (N // P) * CHUNK
RAW_BYTES = 4 * 2 * PASS
ROWS1_AT = RES_BYTES
RES_AT = (0, ROWS1_AT + 2 * PASS)
LIVE = 96


def tile_list_gmlpt_tanh_mix_res_kernel(
    tc, tab_words, tab_scales, wg_words, wg_scales, wu_words, wu_scales,
    wd8_words, wd8_scales, wd4_words, wd4_scales, res, offs, out,
):
    nc = tc.nc
    mult, add = mybir.AluOpType.mult, mybir.AluOpType.add
    tanh = mybir.ActivationFunctionType.Tanh

    with ExitStack() as ctx:
        keep = ctx.enter_context(tc.tile_pool(name="keep", bufs=1))
        ring = ctx.enter_context(tc.tile_pool(name="ring", bufs=2))
        placed = ctx.enter_context(tc.tile_pool(name="placed", bufs=1))
        psum = ctx.enter_context(tc.psum_pool(name="psum", bufs=8))

        offsets = keep.tile([P, J // 16], U16, name="offsets")
        nc.sync.dma_start(offsets[:], offs)

        w_rows = keep.tile([P, 2, R], U8, name="w_rows", tag="stream2", align_bytes=64)
        nc.vector.memset(w_rows[0:LIVE].rearrange("p w r -> p (w r)").bitcast(I32), 0)
        for w, scales in enumerate((wg_scales, wu_scales)):
            nc.sync.dma_start(w_rows[LIVE:P, w, :].bitcast(I32), scales.rearrange("a q r -> q a r").bitcast(I32))

        tab_rows = keep.tile([P, T], U8, name="tab_rows", align_bytes=64)
        nc.vector.memset(tab_rows[0:LIVE, :].bitcast(I32), 0)
        nc.sync.dma_start(tab_rows[LIVE:P, :].bitcast(I32), tab_scales.rearrange("a q t -> q a t").bitcast(I32))

        table = keep.tile([P, T], U32, name="table", align_bytes=64)
        nc.sync.dma_start(table[:].bitcast(I32), tab_words[0].rearrange("p t b -> p (t b)").bitcast(I32))

        def list_slice(first_chunk, chunks):
            cols = CHUNK // 16
            return offsets[:, first_chunk * cols : (first_chunk + chunks) * cols]

        def spread_rows(rows, width, name, clearer):
            planes = keep.tile([P, 2, width], U8, name=name, align_bytes=64)
            clearer.memset(planes[:].rearrange("p a c -> p (a c)").bitcast(I32), 0)
            for quad in range(4):
                nc.sync.dma_start(
                    planes[32 * quad : 32 * quad + 4].bitcast(I32),
                    rows[LIVE + 8 * quad : LIVE + 8 * quad + 8, :].bitcast(I32),
                )
            return planes

        tab_plane = {}
        w_plane = {}
        wd = {}

        def order_scale_rows(dst, half):
            nc.vector.tensor_copy(
                dst.rearrange("p (w t m) -> p w t m", w=2, t=PACK),
                w_rows[:, :, half * PASS : (half + 1) * PASS].rearrange("p w (m t) -> p w t m", t=PACK),
            )

        def first_planes():
            rows = keep.tile([P, 2 * PASS + CHUNK], U8, name="rows0", tag="rows0", align_bytes=64)
            order_scale_rows(rows[:, 0 : 2 * PASS], 0)
            span = placed.tile([P, 2 * PASS + 128], U8, name="picked_rows0", offset=ROWS1_AT - 64, align_bytes=64)
            picked = span[:, 0:CHUNK]
            nc.vector.tensor_copy(picked, tab_rows[:].indirect(list_slice(0, 1)))
            nc.vector.tensor_copy(rows[:, 2 * PASS :].bitcast(I32), picked.bitcast(I32))
            planes = spread_rows(rows, 2 * PASS + CHUNK, "planes0", nc.vector)
            tab_plane[0] = planes[:, :, 2 * PASS :]
            for w in range(2):
                w_plane[w, 0] = planes[:, :, w * PASS : (w + 1) * PASS]

        def second_planes():
            rows = placed.tile([P, 2 * PASS], U8, name="rows1", offset=ROWS1_AT, align_bytes=64)
            order_scale_rows(rows[:], 1)
            planes = spread_rows(rows, 2 * PASS, "planes1", nc.gpsimd)
            for w in range(2):
                w_plane[w, 1] = planes[:, :, w * PASS : (w + 1) * PASS]

        def late_planes():
            width = (CHUNKS - 1) * CHUNK
            picked = placed.tile([P, width], U8, name="picked_rows1", offset=RES_AT[1], align_bytes=64)
            nc.vector.tensor_copy(picked[:], tab_rows[:].indirect(list_slice(1, CHUNKS - 1)))
            rows = keep.tile([P, width + N], U8, name="rows2", tag="rows0", align_bytes=64)
            for half, scales in enumerate((wd8_scales, wd4_scales)):
                nc.sync.dma_start(rows[LIVE + half : P : 2, width:].bitcast(I32), scales[0].bitcast(I32))
            nc.vector.tensor_copy(rows[:, 0:width].bitcast(I32), picked[:].bitcast(I32))
            planes = spread_rows(rows, width + N, "planes2", nc.gpsimd)
            wd["planes"] = planes[:, :, width:]
            for c in range(1, CHUNKS):
                tab_plane[c] = planes[:, :, (c - 1) * CHUNK : c * CHUNK]

        w_codes = {}

        def load_weights(w, half, raw):
            words = (wg_words, wu_words)[w]
            src = words.rearrange("a p r i -> p a (r i)")[:, :, half * PASS * 4 : (half + 1) * PASS * 4]
            nc.sync.dma_start(raw, src.bitcast(I32))

        def order_weights(w, half, raw, a0):
            passes = raw.shape[1]
            codes = keep.tile([P, passes, PASS], I32, name="w_codes%d%d%d" % (w, half, a0), align_bytes=64)
            nc.vector.tensor_copy(
                codes[:].rearrange("p a (t g i) -> p a g t i", t=PACK, i=4),
                raw.rearrange("p a (g i t) -> p a g t i", t=PACK, i=4),
            )
            for a in range(passes):
                w_codes[w, half, a0 + a] = codes[:, a, :]

        tab_codes = {}

        def pick_words(c):
            picked = keep.tile([P, CHUNK], U32, name="picked_words", tag="stream2" if c > 0 else "picked_words0", align_bytes=64)
            nc.vector.tensor_copy(picked[:], table[:].indirect(list_slice(c, 1)))
            parted = ring.tile([P, 2, 2 * CHUNK], U8, name="parted", align_bytes=64)
            nc.vector.tensor_copy(parted[:].bitcast(U16), picked[:].bitcast(U16).rearrange("p (j a) -> p a j", a=2))
            tab_codes[c] = parted

        def load_down():
            words = keep.tile([P, 6 * N], U8, name="wd_words", tag="picked_words0", align_bytes=64)
            wd8, wd4 = words[:, 0 : 4 * N], words[:, 4 * N :]
            nc.sync.dma_start(wd8.bitcast(I32), wd8_words[0].rearrange("p n i -> p (n i)").bitcast(I32))
            nc.sync.dma_start(wd4.bitcast(I32), wd4_words[0].bitcast(I32))
            wd["codes"] = (wd8, wd4)

        res_tiles = {}

        def load_res(c):
            tile = placed.tile([P, N // P, CHUNK], F32, name="res_tile", tag="res%d" % (c % 2), offset=RES_AT[c % 2], align_bytes=64)
            nc.sync.dma_start(tile[:], res[:, c * CHUNK : (c + 1) * CHUNK].rearrange("(b p) j -> p b j", p=P))
            res_tiles[c] = tile

        def first_product(dst, w, half, t, c, j0, width):
            for a in range(2):
                nc.tensor.matmul_mx(
                    out=dst,
                    lhsT=w_codes[w, half, a][:, t * P : (t + 1) * P].bitcast(FP8X4),
                    lhsT_scale=w_plane[w, half][:, a, t * P : (t + 1) * P],
                    rhs=tab_codes[c][:, a, 2 * j0 : 2 * (j0 + width)].bitcast(FP4X4),
                    rhs_scale=tab_plane[c][:, a, j0 : j0 + width],
                    start=(a == 0),
                    stop=(a == 1),
                )

        def gate(c, half):
            gates = ring.tile([P, PACK, CHUNK], F32, name="gates")
            for t in range(PACK):
                bank = psum.tile([P, CHUNK], F32, name="bank")
                first_product(bank[:], 0, half, t, c, 0, CHUNK)
                nc.scalar.activation(gates[:, t, :], bank[:], tanh)
            return gates

        def up_times_gate(c, half, s, gates, h):
            bank = psum.tile([P, CHUNK], F32, name="bank")
            for t in range(PACK):
                first_product(bank[:, t * SUB : (t + 1) * SUB], 1, half, t, c, s * SUB, SUB)
            nc.vector.tensor_tensor(
                h[:, s * SUB * PACK : (s + 1) * SUB * PACK].rearrange("p (g i t) -> p g t i", t=PACK, i=2),
                bank[:].rearrange("p (t g i) -> p g t i", t=PACK, i=2),
                gates[:, :, s * SUB : (s + 1) * SUB].rearrange("p t (g i) -> p g t i", i=2),
                mult,
            )

        def up_then_product(c, half, gates, h):
            ups = ring.tile([P, PACK, CHUNK], F32, name="ups")
            for t in range(PACK):
                bank = psum.tile([P, CHUNK], F32, name="bank")
                first_product(bank[:], 1, half, t, c, 0, CHUNK)
                nc.scalar.copy(ups[:, t, :], bank[:])
            nc.vector.tensor_tensor(
                h[:].rearrange("p (g i t) -> p g t i", t=PACK, i=2),
                ups[:].rearrange("p t (g i) -> p g t i", i=2),
                gates[:].rearrange("p t (g i) -> p g t i", i=2),
                mult,
            )

        h_codes = {}

        def new_h(c, half):
            h = ring.tile([P, CHUNK * PACK], BF16, name="h", align_bytes=64)
            codes = ring.tile([P, CHUNK], U32, name="h_words", tag="h_words%d" % half, align_bytes=64)
            scales = ring.tile([P, CHUNK], U8, name="h_scales", tag="h_scales%d" % half, align_bytes=64)
            h_codes[c, half] = (codes, scales)
            return h

        def quantise(c, half, h, j0, width):
            codes, scales = h_codes[c, half]
            nc.vector.quantize_mx(
                out=codes[:, j0 : j0 + width].bitcast(FP8X4),
                scales=scales[:, j0 : j0 + width],
                in_=h[:, j0 * PACK : (j0 + width) * PACK],
            )

        def second_product(dst, c, b, j0, width):
            wd8, wd4 = wd["codes"]
            stationary = (wd8[:, 4 * b * P : 4 * (b + 1) * P].bitcast(FP8X4), wd4[:, 2 * b * P : 2 * (b + 1) * P].bitcast(FP4X4))
            for half in range(HALVES):
                codes, scales = h_codes[c, half]
                nc.tensor.matmul_mx(
                    out=dst,
                    lhsT=stationary[half],
                    lhsT_scale=wd["planes"][:, half, b * P : (b + 1) * P],
                    rhs=codes[:, j0 : j0 + width].bitcast(FP8X4),
                    rhs_scale=scales[:, j0 : j0 + width],
                    start=(half == 0),
                    stop=(half == HALVES - 1),
                )

        def down(c):
            for b in range(N // P):
                bank = psum.tile([P, CHUNK], F32, name="bank")
                second_product(bank[:], c, b, 0, CHUNK)
                result = ring.tile([P, CHUNK], F32, name="result", bufs=4)
                nc.vector.tensor_tensor(result[:], bank[:], res_tiles[c][:, b, :], add)
                nc.sync.dma_start(out[b * P : (b + 1) * P, c * CHUNK : (c + 1) * CHUNK], result[:])

        def down_sub(c, s):
            bank = psum.tile([P, CHUNK], F32, name="bank")
            for b in range(N // P):
                second_product(bank[:, b * SUB : (b + 1) * SUB], c, b, s * SUB, SUB)
            j0 = c * CHUNK + s * SUB
            sums = bank[:].rearrange("p (b j) -> p b j", j=SUB)
            stored = out[:, j0 : j0 + SUB].rearrange("(b p) j -> p b j", p=P)
            queues = (nc.sync, nc.scalar) if s == SUBS - 1 else (nc.sync,)
            blocks = N // P // len(queues)
            for n, queue in enumerate(queues):
                part = slice(n * blocks, (n + 1) * blocks)
                result = ring.tile([P, blocks, SUB], F32, name="result", bufs=4)
                nc.vector.tensor_tensor(result[:], sums[:, part], res_tiles[c][:, part, s * SUB : (s + 1) * SUB], add)
                queue.dma_start(stored[:, part], result[:])

        first_planes()
        raw_gate0 = placed.tile([P, 2, PASS], I32, name="raw_gate0", offset=RES_BYTES - RAW_BYTES, align_bytes=64)
        load_weights(0, 0, raw_gate0[:])
        raw_up0 = placed.tile([P, 2, PASS], I32, name="raw_up0", offset=RES_AT[1], align_bytes=64)
        load_weights(1, 0, raw_up0[:])
        second_planes()
        raw1 = keep.tile([P, 2, 2, PASS], I32, name="raw1", tag="stream2", align_bytes=64)
        for w in range(2):
            load_weights(w, 1, raw1[:, w])
        pick_words(0)
        for a in range(2):
            order_weights(0, 0, raw_gate0[:, a : a + 1, :], a)
        order_weights(1, 0, raw_up0[:], 0)
        for w in range(2):
            order_weights(w, 1, raw1[:, w], 0)
        late_planes()
        load_down()

        for c in range(CHUNKS):
            last = c == CHUNKS - 1
            load_res(c)
            for half in range(HALVES):
                gates = gate(c, half)
                if half == 1 and c > 0:
                    down(c - 1)
                if half == 1 and not last:
                    pick_words(c + 1)
                h = new_h(c, half)
                if last and half == 1:
                    for s in range(SUBS + 2):
                        if s < SUBS:
                            up_times_gate(c, half, s, gates, h)
                            quantise(c, half, h, s * SUB, SUB)
                        if s >= 2:
                            down_sub(c, s - 2)
                else:
                    up_then_product(c, half, gates, h)
                    quantise(c, half, h, 0, CHUNK)
